import numpy as np
import ml_dtypes


def mxq(x, axis, fmt="e4m3"):
    dtype, down = {"e4m3": (ml_dtypes.float8_e4m3fn, 7), "e5m2": (ml_dtypes.float8_e5m2, 14)}[fmt]
    v = np.moveaxis(np.asarray(x, np.float32).astype(ml_dtypes.bfloat16).astype(np.float64), axis, -1)
    blocks = v.reshape(v.shape[:-1] + (-1, 32))
    amax = np.abs(blocks).max(-1, keepdims=True)
    byte = np.maximum(np.where(amax > 0, np.frexp(amax)[1] - 1 + 127, 0) - down, 1)
    scale = np.exp2(byte - 127.0)
    codes = (blocks / scale).astype(np.float32).astype(dtype).astype(np.float64)
    return np.moveaxis((codes * scale).reshape(v.shape), -1, axis)


WIDE = False


def mx_kscale(k, group=512):
    if not WIDE:
        return np.ones(k)
    levels = np.array([18, -18])
    if group != 512:
        return np.exp2(np.random.permutation(np.resize(levels, k // group))).repeat(group)
    if k % 512:
        return np.exp2(np.random.permutation(np.resize(levels, k // 32))).repeat(32)
    a = np.empty((k // 512, 16))
    for p in range(k // 512):
        a[p, :8] = np.random.permutation(np.resize(levels, 8))
        for g in range(8):
            far = levels[np.abs(levels - a[p, g]) >= 10]
            a[p, g + 8] = far[np.random.randint(len(far))]
    return np.exp2(a.ravel()).repeat(32)


def f64(x):
    return np.asarray(x).astype(np.float64)


G, D, M, N = 4, 128, 128, 512


def setup_inputs():
    n = np.random.standard_normal
    s_d = mx_kscale(D, 0)
    return {
        "x": (n((G, D, N)) * s_d[:, None]).astype(np.float32),
        "w1": (n((G, D, M)) / np.sqrt(D) / s_d[:, None]).astype(np.float32),
        "w2": (n((G, D, M)) / np.sqrt(D) / s_d[:, None]).astype(np.float32),
        "so": (np.random.uniform(0.3, 1.0, (G, M, 1))).astype(np.float32),
        "dx": (n((G, D, N)) * s_d[:, None]).astype(np.float32),
        "og": (np.random.uniform(0.5, 2.0, (G, M, 1))).astype(np.float32),
        "base": (0.3 * n((G, M, N))).astype(np.float32),
    }


def reference(x, w1, w2, so, dx, og, base):
    w1q = mxq(f64(w1), 1, "e4m3")
    xq = mxq(f64(x), 1, "e4m3")
    z1 = w1q.transpose(0, 2, 1) @ xq
    dxq = mxq(f64(dx), 1, "e4m3")
    tz1 = w1q.transpose(0, 2, 1) @ dxq
    w2q = mxq(f64(w2), 1, "e4m3")
    z2 = w2q.transpose(0, 2, 1) @ xq
    tz2 = w2q.transpose(0, 2, 1) @ dxq
    nm = np.sqrt(np.square(z1) * np.square(z2) + f64(so))
    xnm = (tz1 * z1 * 2.0 * np.square(z2) + tz2 * z2 * 2.0 * np.square(z1)) * 0.5 / nm
    xh = (tz1 * z2 + tz2 * z1 - xnm * z1 * z2 / nm) / nm
    y = xh * f64(og) + f64(base)
    return y

@@ -1,0 +1,174 @@
+from contextlib import ExitStack
+
+import concourse.mybir as mybir
+
+G, D, M, N = 4, 128, 128, 512
+FLOPS = 4 * 2 * G * D * M * N
+
+F32 = mybir.dt.float32
+BF16 = mybir.dt.bfloat16
+U32 = mybir.dt.uint32
+U8 = mybir.dt.uint8
+FP8X4 = mybir.dt.float8_e4m3fn_x4
+ACT = mybir.ActivationFunctionType
+ALU = mybir.AluOpType
+
+P = 128
+PACK = 4
+ROWS = D // PACK
+X_SPLIT = 344
+
+
+def interleave(copy, raw, grouped, c0, c1):
+    copy(
+        out=grouped[:, c0:c1, :].rearrange("p (c i) j -> p c j i", i=4),
+        in_=raw[:, :, c0:c1].rearrange("p j (c i) -> p c j i", i=4),
+    )
+
+
+def tile_rows_tnagree_kernel(tc, x, w1, w2, so, dx, og, base, out):
+    nc = tc.nc
+    with ExitStack() as ctx:
+        sb = ctx.enter_context(tc.tile_pool(name="sb", bufs=1))
+        ps = ctx.enter_context(tc.psum_pool(name="ps", bufs=1))
+        ctx.enter_context(tc.manual_schedule())
+
+        def operand(name, width):
+            raw = sb.tile([P, PACK, width], F32, name=name + "_raw", align_bytes=64)
+            grouped = sb.tile([P, width, PACK], BF16, name=name + "_bf", align_bytes=64)
+            codes = sb.tile([P, width], U32, name=name + "_codes", align_bytes=64)
+            scales = sb.tile([P, width], U8, name=name + "_scales", align_bytes=64)
+            return raw, grouped, codes, scales
+
+        xq, dxq = operand("x", N), operand("dx", N)
+        w1q, w2q = operand("w1", M), operand("w2", M)
+
+        def load(src, opnd):
+            nc.sync.dma_start(out=opnd[0][:], in_=src.rearrange("g (p j) n -> (g p) j n", j=PACK))
+
+        def quantize(opnd):
+            nc.vector.quantize_mx(
+                out=opnd[2][:].bitcast(FP8X4),
+                scales=opnd[3][:],
+                in_=opnd[1][:].rearrange("p n j -> p (n j)"),
+            )
+
+        def product(bank, w, act, g):
+            rows = slice(ROWS * g, ROWS * (g + 1))
+            nc.tensor.matmul_mx(
+                out=bank[:],
+                lhsT=w[2][rows, :].bitcast(FP8X4),
+                lhsT_scale=w[3][rows, :],
+                rhs=act[2][rows, :].bitcast(FP8X4),
+                rhs_scale=act[3][rows, :],
+                start=True,
+                stop=True,
+            )
+
+        def per_group(name):
+            return [sb.tile([P, N], F32, name=name + str(g), align_bytes=64) for g in range(G)]
+
+        bank1 = [ps.tile([M, N], F32, name="bank1_" + str(g)) for g in range(G)]
+        bank2 = [ps.tile([M, N], F32, name="bank2_" + str(g)) for g in range(G)]
+        z1, z2, prod, sq, lg = (per_group(n) for n in ("z1_", "z2_", "prod", "sq", "lg"))
+        u, v, tp, r3, t, y = (per_group(n) for n in ("u", "v", "tp", "r3_", "t", "y"))
+        base_sb = sb.tile([P, G, N], F32)
+        feat_rows = sb.tile([P, 2 * M], F32, align_bytes=64)
+        feat_cols = sb.tile([P, 2 * M], F32, align_bytes=64)
+        gain = sb.tile([P, G], F32)
+        warm = sb.tile([P, 8], F32)
+
+        load(x, xq)
+        load(w1, w1q)
+        load(w2, w2q)
+        load(dx, dxq)
+        nc.sync.dma_start(out=base_sb[:], in_=base.rearrange("g m n -> m g n"))
+
+        nc.vector.memset(feat_rows[:], 0.0)
+        nc.vector.memset(warm[:], 1.0)
+        for k, vec in enumerate((so, og)):
+            nc.scalar.dma_start(
+                out=feat_rows[0:P:32, k * M : (k + 1) * M].rearrange("q (g i) -> q g i", g=G),
+                in_=vec.rearrange("g (q i) o -> q g (i o)", i=32),
+            )
+        nc.scalar.activation(out=warm[:, 4:5], in_=warm[:, 0:1], func=ACT.Ln)
+
+        interleave(nc.vector.tensor_copy, xq[0], xq[1], 0, X_SPLIT)
+        interleave(nc.scalar.copy, xq[0], xq[1], X_SPLIT, N)
+        interleave(nc.scalar.copy, w1q[0], w1q[1], 0, M)
+        interleave(nc.scalar.copy, w2q[0], w2q[1], 0, M)
+        quantize(xq)
+        quantize(w1q)
+        quantize(w2q)
+        nc.vector.transpose(out=feat_cols[:], in_=feat_rows[:])
+
+        def so_col(g):
+            return feat_cols[:, 32 * g : 32 * g + 1]
+
+        def view1(g):
+            product(bank1[g], w1q, xq, g)
+            nc.scalar.copy(out=z1[g][:], in_=bank1[g][:])
+
+        def view2(g):
+            product(bank2[g], w2q, xq, g)
+            nc.vector.tensor_tensor(out=prod[g][:], in0=bank2[g][:], in1=z1[g][:], op=ALU.mult)
+            nc.scalar.copy(out=z2[g][:], in_=bank2[g][:])
+
+        view1(0)
+        view1(1)
+        view2(0)
+        nc.vector.tensor_tensor(
+            out=gain[:], in0=feat_cols[:, 0:M:32], in1=feat_cols[:, M : 2 * M : 32], op=ALU.mult
+        )
+        view1(2)
+        view2(1)
+        interleave(nc.vector.tensor_copy, dxq[0], dxq[1], 0, N)
+        view1(3)
+        view2(2)
+        quantize(dxq)
+        view2(3)
+
+        def square(g):
+            nc.scalar.activation(out=sq[g][:], in_=prod[g][:], func=ACT.Square)
+
+        def logarithm(g):
+            nc.scalar.activation(out=lg[g][:], in_=sq[g][:], func=ACT.Ln, bias=so_col(g))
+
+        def power(g):
+            nc.scalar.activation(out=r3[g][:], in_=lg[g][:], func=ACT.Exp, scale=-1.5)
+
+        square(0)
+        for g in range(G):
+            if g + 1 < G:
+                square(g + 1)
+            logarithm(g)
+        for g in range(G):
+            power(g)
+
+        def tangents(g):
+            product(bank1[g], w1q, dxq, g)
+            product(bank2[g], w2q, dxq, g)
+            nc.vector.tensor_tensor(out=v[g][:], in0=bank1[g][:], in1=z2[g][:], op=ALU.mult)
+            nc.vector.tensor_tensor(out=u[g][:], in0=bank2[g][:], in1=z1[g][:], op=ALU.mult)
+
+        def tangent_sum(g):
+            nc.vector.tensor_tensor(out=tp[g][:], in0=u[g][:], in1=v[g][:], op=ALU.add)
+
+        def weigh(g):
+            nc.vector.scalar_tensor_tensor(
+                out=t[g][:], in0=tp[g][:], scalar=gain[:, g : g + 1], in1=r3[g][:], op0=ALU.mult, op1=ALU.mult
+            )
+
+        def finish(g):
+            nc.vector.tensor_tensor(out=y[g][:], in0=t[g][:], in1=base_sb[:, g, :], op=ALU.add)
+            nc.sync.dma_start(out=out[g], in_=y[g][:])
+
+        for g in range(G):
+            tangents(g)
+        for g in range(G):
+            tangent_sum(g)
+        weigh(0)
+        for g in range(G):
+            if g + 1 < G:
+                weigh(g + 1)
+            finish(g)

@@ -16,14 +16,8 @@ ALU = mybir.AluOpType
 P = 128
 PACK = 4
 ROWS = D // PACK
-X_SPLIT = 344
-
-
-def interleave(copy, raw, grouped, c0, c1):
-    copy(
-        out=grouped[:, c0:c1, :].rearrange("p (c i) j -> p c j i", i=4),
-        in_=raw[:, :, c0:c1].rearrange("p j (c i) -> p c j i", i=4),
-    )
+HALF = N // 2
+X_SPLIT = 168
 
 
 def tile_rows_tnagree_kernel(tc, x, w1, w2, so, dx, og, base, out):
@@ -33,24 +27,38 @@ def tile_rows_tnagree_kernel(tc, x, w1, w2, so, dx, og, base, out):
         ps = ctx.enter_context(tc.psum_pool(name="ps", bufs=1))
         ctx.enter_context(tc.manual_schedule())
 
-        def operand(name, width):
-            raw = sb.tile([P, PACK, width], F32, name=name + "_raw", align_bytes=64)
+        def operand(name, width, parts):
+            raws = [
+                sb.tile([P, PACK, width // parts], F32, name=name + "_raw" + str(h), align_bytes=64)
+                for h in range(parts)
+            ]
             grouped = sb.tile([P, width, PACK], BF16, name=name + "_bf", align_bytes=64)
             codes = sb.tile([P, width], U32, name=name + "_codes", align_bytes=64)
             scales = sb.tile([P, width], U8, name=name + "_scales", align_bytes=64)
-            return raw, grouped, codes, scales
+            return raws, grouped, codes, scales
 
-        xq, dxq = operand("x", N), operand("dx", N)
-        w1q, w2q = operand("w1", M), operand("w2", M)
+        xq, dxq = operand("x", N, 2), operand("dx", N, 2)
+        w1q, w2q = operand("w1", M, 1), operand("w2", M, 1)
 
-        def load(src, opnd):
-            nc.sync.dma_start(out=opnd[0][:], in_=src.rearrange("g (p j) n -> (g p) j n", j=PACK))
+        def load(src, opnd, h):
+            width = opnd[0][h].shape[2]
+            rows = src.rearrange("g (p j) n -> (g p) j n", j=PACK)
+            nc.sync.dma_start(out=opnd[0][h][:], in_=rows[:, :, h * width : (h + 1) * width])
 
-        def quantize(opnd):
+        def interleave(copy, opnd, h, c0, c1):
+            first = h * opnd[0][h].shape[2]
+            copy(
+                out=opnd[1][:, first + c0 : first + c1, :].rearrange("p (c i) j -> p c j i", i=4),
+                in_=opnd[0][h][:, :, c0:c1].rearrange("p j (c i) -> p c j i", i=4),
+            )
+
+        def quantize(opnd, h):
+            width = opnd[0][h].shape[2]
+            cols = slice(h * width, (h + 1) * width)
             nc.vector.quantize_mx(
-                out=opnd[2][:].bitcast(FP8X4),
-                scales=opnd[3][:],
-                in_=opnd[1][:].rearrange("p n j -> p (n j)"),
+                out=opnd[2][:, cols].bitcast(FP8X4),
+                scales=opnd[3][:, cols],
+                in_=opnd[1][:, cols, :].rearrange("p n j -> p (n j)"),
             )
 
         def product(bank, w, act, g):
@@ -78,55 +86,69 @@ def tile_rows_tnagree_kernel(tc, x, w1, w2, so, dx, og, base, out):
         gain = sb.tile([P, G], F32)
         warm = sb.tile([P, 8], F32)
 
-        load(x, xq)
-        load(w1, w1q)
-        load(w2, w2q)
-        load(dx, dxq)
-        nc.sync.dma_start(out=base_sb[:], in_=base.rearrange("g m n -> m g n"))
-
         nc.vector.memset(feat_rows[:], 0.0)
         nc.vector.memset(warm[:], 1.0)
+        load(w1, w1q, 0)
+        load(x, xq, 0)
         for k, vec in enumerate((so, og)):
-            nc.scalar.dma_start(
+            nc.sync.dma_start(
                 out=feat_rows[0:P:32, k * M : (k + 1) * M].rearrange("q (g i) -> q g i", g=G),
                 in_=vec.rearrange("g (q i) o -> q g (i o)", i=32),
             )
+        load(x, xq, 1)
+        load(w2, w2q, 0)
+        load(dx, dxq, 0)
+        load(dx, dxq, 1)
+        nc.sync.dma_start(out=base_sb[:], in_=base.rearrange("g m n -> m g n"))
+
         nc.scalar.activation(out=warm[:, 4:5], in_=warm[:, 0:1], func=ACT.Ln)
 
-        interleave(nc.vector.tensor_copy, xq[0], xq[1], 0, X_SPLIT)
-        interleave(nc.scalar.copy, xq[0], xq[1], X_SPLIT, N)
-        interleave(nc.scalar.copy, w1q[0], w1q[1], 0, M)
-        interleave(nc.scalar.copy, w2q[0], w2q[1], 0, M)
-        quantize(xq)
-        quantize(w1q)
-        quantize(w2q)
-        nc.vector.transpose(out=feat_cols[:], in_=feat_rows[:])
+        interleave(nc.vector.tensor_copy, w1q, 0, 0, M)
+        quantize(w1q, 0)
+        for h in range(2):
+            interleave(nc.vector.tensor_copy, xq, h, 0, X_SPLIT)
+            interleave(nc.scalar.copy, xq, h, X_SPLIT, HALF)
+            if h == 0:
+                nc.vector.transpose(out=feat_cols[:], in_=feat_rows[:])
+            quantize(xq, h)
+        interleave(nc.scalar.copy, w2q, 0, 0, M)
+        nc.vector.tensor_tensor(
+            out=gain[:], in0=feat_cols[:, 0:M:32], in1=feat_cols[:, M : 2 * M : 32], op=ALU.mult
+        )
+        quantize(w2q, 0)
+        for h in range(2):
+            interleave(nc.vector.tensor_copy, dxq, h, 0, HALF)
+            quantize(dxq, h)
 
         def so_col(g):
             return feat_cols[:, 32 * g : 32 * g + 1]
 
-        def view1(g):
-            product(bank1[g], w1q, xq, g)
-            nc.scalar.copy(out=z1[g][:], in_=bank1[g][:])
+        pairs = [(0, 1), (2, 3)]
+        for pair in pairs:
+            for banks, w, z in ((bank1, w1q, z1), (bank2, w2q, z2)):
+                for g in pair:
+                    product(banks[g], w, xq, g)
+                    nc.scalar.copy(out=z[g][:], in_=banks[g][:])
 
-        def view2(g):
-            product(bank2[g], w2q, xq, g)
-            nc.vector.tensor_tensor(out=prod[g][:], in0=bank2[g][:], in1=z1[g][:], op=ALU.mult)
-            nc.scalar.copy(out=z2[g][:], in_=bank2[g][:])
+        def views_product(g):
+            nc.vector.tensor_tensor(out=prod[g][:], in0=z1[g][:], in1=z2[g][:], op=ALU.mult)
 
-        view1(0)
-        view1(1)
-        view2(0)
-        nc.vector.tensor_tensor(
-            out=gain[:], in0=feat_cols[:, 0:M:32], in1=feat_cols[:, M : 2 * M : 32], op=ALU.mult
-        )
-        view1(2)
-        view2(1)
-        interleave(nc.vector.tensor_copy, dxq[0], dxq[1], 0, N)
-        view1(3)
-        view2(2)
-        quantize(dxq)
-        view2(3)
+        def cross(banks, w, z, dst, g):
+            product(banks[g], w, dxq, g)
+            nc.vector.tensor_tensor(out=dst[g][:], in0=banks[g][:], in1=z[g][:], op=ALU.mult)
+
+        for pair in pairs:
+            for g in pair:
+                views_product(g)
+            if pair == pairs[0]:
+                for g in pair:
+                    cross(bank1, w1q, z2, v, g)
+        for g in pairs[0]:
+            cross(bank2, w2q, z1, u, g)
+        for g in pairs[1]:
+            cross(bank1, w1q, z2, v, g)
+        for g in pairs[1]:
+            cross(bank2, w2q, z1, u, g)
 
         def square(g):
             nc.scalar.activation(out=sq[g][:], in_=prod[g][:], func=ACT.Square)
@@ -145,30 +167,33 @@ def tile_rows_tnagree_kernel(tc, x, w1, w2, so, dx, og, base, out):
         for g in range(G):
             power(g)
 
-        def tangents(g):
-            product(bank1[g], w1q, dxq, g)
-            product(bank2[g], w2q, dxq, g)
-            nc.vector.tensor_tensor(out=v[g][:], in0=bank1[g][:], in1=z2[g][:], op=ALU.mult)
-            nc.vector.tensor_tensor(out=u[g][:], in0=bank2[g][:], in1=z1[g][:], op=ALU.mult)
-
         def tangent_sum(g):
             nc.vector.tensor_tensor(out=tp[g][:], in0=u[g][:], in1=v[g][:], op=ALU.add)
 
-        def weigh(g):
+        def weigh(g, c0, c1):
             nc.vector.scalar_tensor_tensor(
-                out=t[g][:], in0=tp[g][:], scalar=gain[:, g : g + 1], in1=r3[g][:], op0=ALU.mult, op1=ALU.mult
+                out=t[g][:, c0:c1],
+                in0=tp[g][:, c0:c1],
+                scalar=gain[:, g : g + 1],
+                in1=r3[g][:, c0:c1],
+                op0=ALU.mult,
+                op1=ALU.mult,
             )
 
-        def finish(g):
-            nc.vector.tensor_tensor(out=y[g][:], in0=t[g][:], in1=base_sb[:, g, :], op=ALU.add)
-            nc.sync.dma_start(out=out[g], in_=y[g][:])
+        def finish(g, c0, c1):
+            nc.vector.tensor_tensor(out=y[g][:, c0:c1], in0=t[g][:, c0:c1], in1=base_sb[:, g, c0:c1], op=ALU.add)
+            nc.sync.dma_start(out=out[g, :, c0:c1], in_=y[g][:, c0:c1])
 
         for g in range(G):
-            tangents(g)
-        for g in range(G):
             tangent_sum(g)
-        weigh(0)
-        for g in range(G):
-            if g + 1 < G:
-                weigh(g + 1)
-            finish(g)
+        last = G - 1
+        weigh(0, 0, N)
+        for g in range(last):
+            if g + 1 < last:
+                weigh(g + 1, 0, N)
+            else:
+                weigh(last, 0, HALF)
+            finish(g, 0, N)
+        weigh(last, HALF, N)
+        finish(last, 0, HALF)
+        finish(last, HALF, N)

@@ -123,35 +123,18 @@ def tile_rows_tnagree_kernel(tc, x, w1, w2, so, dx, og, base, out):
         def so_col(g):
             return feat_cols[:, 32 * g : 32 * g + 1]
 
-        pairs = [(0, 1), (2, 3)]
-        for pair in pairs:
-            for banks, w, z in ((bank1, w1q, z1), (bank2, w2q, z2)):
-                for g in pair:
-                    product(banks[g], w, xq, g)
-                    nc.scalar.copy(out=z[g][:], in_=banks[g][:])
+        for g in range(G):
+            product(bank1[g], w1q, xq, g)
+            nc.scalar.copy(out=z1[g][:], in_=bank1[g][:])
+        for g in range(G):
+            product(bank2[g], w2q, xq, g)
+            nc.vector.tensor_tensor(out=prod[g][:], in0=bank2[g][:], in1=z1[g][:], op=ALU.mult)
+            nc.scalar.copy(out=z2[g][:], in_=bank2[g][:])
 
-        def views_product(g):
-            nc.vector.tensor_tensor(out=prod[g][:], in0=z1[g][:], in1=z2[g][:], op=ALU.mult)
-
-        def cross(banks, w, z, dst, g):
-            product(banks[g], w, dxq, g)
-            nc.vector.tensor_tensor(out=dst[g][:], in0=banks[g][:], in1=z[g][:], op=ALU.mult)
-
-        for pair in pairs:
-            for g in pair:
-                views_product(g)
-            if pair == pairs[0]:
-                for g in pair:
-                    cross(bank1, w1q, z2, v, g)
-        for g in pairs[0]:
-            cross(bank2, w2q, z1, u, g)
-        for g in pairs[1]:
-            cross(bank1, w1q, z2, v, g)
-        for g in pairs[1]:
-            cross(bank2, w2q, z1, u, g)
-
-        def square(g):
-            nc.scalar.activation(out=sq[g][:], in_=prod[g][:], func=ACT.Square)
+        def cross(g):
+            for banks, w, z, dst in ((bank1, w1q, z2, v), (bank2, w2q, z1, u)):
+                product(banks[g], w, dxq, g)
+                nc.vector.tensor_tensor(out=dst[g][:], in0=banks[g][:], in1=z[g][:], op=ALU.mult)
 
         def logarithm(g):
             nc.scalar.activation(out=lg[g][:], in_=sq[g][:], func=ACT.Ln, bias=so_col(g))
@@ -159,16 +142,23 @@ def tile_rows_tnagree_kernel(tc, x, w1, w2, so, dx, og, base, out):
         def power(g):
             nc.scalar.activation(out=r3[g][:], in_=lg[g][:], func=ACT.Exp, scale=-1.5)
 
-        square(0)
+        def tangent_sum(engine, g):
+            engine.tensor_tensor(out=tp[g][:], in0=u[g][:], in1=v[g][:], op=ALU.add)
+
         for g in range(G):
-            if g + 1 < G:
-                square(g + 1)
-            logarithm(g)
+            cross(g)
+
+        for g in range(G - 1):
+            nc.gpsimd.tensor_tensor(out=sq[g][:], in0=prod[g][:], in1=prod[g][:], op=ALU.mult)
+        logarithm(0)
+        nc.scalar.activation(out=sq[G - 1][:], in_=prod[G - 1][:], func=ACT.Square)
+        logarithm(1)
+        logarithm(3)
+        logarithm(2)
         for g in range(G):
             power(g)
-
-        def tangent_sum(g):
-            nc.vector.tensor_tensor(out=tp[g][:], in0=u[g][:], in1=v[g][:], op=ALU.add)
+        for g in range(G):
+            tangent_sum(nc.gpsimd if g < 2 else nc.vector, g)
 
         def weigh(g, c0, c1):
             nc.vector.scalar_tensor_tensor(
@@ -184,8 +174,6 @@ def tile_rows_tnagree_kernel(tc, x, w1, w2, so, dx, og, base, out):
             nc.vector.tensor_tensor(out=y[g][:, c0:c1], in0=t[g][:, c0:c1], in1=base_sb[:, g, c0:c1], op=ALU.add)
             nc.sync.dma_start(out=out[g, :, c0:c1], in_=y[g][:, c0:c1])
 
-        for g in range(G):
-            tangent_sum(g)
         last = G - 1
         weigh(0, 0, N)
         for g in range(last):

@@ -17,7 +17,7 @@ P = 128
 PACK = 4
 ROWS = D // PACK
 HALF = N // 2
-X_SPLIT = 168
+X_SPLIT = 344
 
 
 def tile_rows_tnagree_kernel(tc, x, w1, w2, so, dx, og, base, out):
@@ -29,7 +29,7 @@ def tile_rows_tnagree_kernel(tc, x, w1, w2, so, dx, og, base, out):
 
         def operand(name, width, parts):
             raws = [
-                sb.tile([P, PACK, width // parts], F32, name=name + "_raw" + str(h), align_bytes=64)
+                sb.tile([P, PACK // parts, width], F32, name=name + "_raw" + str(h), align_bytes=64)
                 for h in range(parts)
             ]
             grouped = sb.tile([P, width, PACK], BF16, name=name + "_bf", align_bytes=64)
@@ -41,24 +41,22 @@ def tile_rows_tnagree_kernel(tc, x, w1, w2, so, dx, og, base, out):
         w1q, w2q = operand("w1", M, 1), operand("w2", M, 1)
 
         def load(src, opnd, h):
-            width = opnd[0][h].shape[2]
+            places = opnd[0][h].shape[1]
             rows = src.rearrange("g (p j) n -> (g p) j n", j=PACK)
-            nc.sync.dma_start(out=opnd[0][h][:], in_=rows[:, :, h * width : (h + 1) * width])
+            nc.sync.dma_start(out=opnd[0][h][:], in_=rows[:, h * places : (h + 1) * places, :])
 
         def interleave(copy, opnd, h, c0, c1):
-            first = h * opnd[0][h].shape[2]
+            places = opnd[0][h].shape[1]
             copy(
-                out=opnd[1][:, first + c0 : first + c1, :].rearrange("p (c i) j -> p c j i", i=4),
+                out=opnd[1][:, c0:c1, h * places : (h + 1) * places].rearrange("p (c i) j -> p c j i", i=4),
                 in_=opnd[0][h][:, :, c0:c1].rearrange("p j (c i) -> p c j i", i=4),
             )
 
-        def quantize(opnd, h):
-            width = opnd[0][h].shape[2]
-            cols = slice(h * width, (h + 1) * width)
+        def quantize(opnd):
             nc.vector.quantize_mx(
-                out=opnd[2][:, cols].bitcast(FP8X4),
-                scales=opnd[3][:, cols],
-                in_=opnd[1][:, cols, :].rearrange("p n j -> p (n j)"),
+                out=opnd[2][:].bitcast(FP8X4),
+                scales=opnd[3][:],
+                in_=opnd[1][:].rearrange("p n j -> p (n j)"),
             )
 
         def product(bank, w, act, g):
@@ -88,7 +86,6 @@ def tile_rows_tnagree_kernel(tc, x, w1, w2, so, dx, og, base, out):
 
         nc.vector.memset(feat_rows[:], 0.0)
         nc.vector.memset(warm[:], 1.0)
-        load(w1, w1q, 0)
         load(x, xq, 0)
         for k, vec in enumerate((so, og)):
             nc.sync.dma_start(
@@ -96,6 +93,7 @@ def tile_rows_tnagree_kernel(tc, x, w1, w2, so, dx, og, base, out):
                 in_=vec.rearrange("g (q i) o -> q g (i o)", i=32),
             )
         load(x, xq, 1)
+        load(w1, w1q, 0)
         load(w2, w2q, 0)
         load(dx, dxq, 0)
         load(dx, dxq, 1)
@@ -103,22 +101,20 @@ def tile_rows_tnagree_kernel(tc, x, w1, w2, so, dx, og, base, out):
 
         nc.scalar.activation(out=warm[:, 4:5], in_=warm[:, 0:1], func=ACT.Ln)
 
-        interleave(nc.vector.tensor_copy, w1q, 0, 0, M)
-        quantize(w1q, 0)
-        for h in range(2):
-            interleave(nc.vector.tensor_copy, xq, h, 0, X_SPLIT)
-            interleave(nc.scalar.copy, xq, h, X_SPLIT, HALF)
-            if h == 0:
-                nc.vector.transpose(out=feat_cols[:], in_=feat_rows[:])
-            quantize(xq, h)
+        interleave(nc.vector.tensor_copy, xq, 0, 0, N)
+        interleave(nc.vector.tensor_copy, xq, 1, 0, X_SPLIT)
+        interleave(nc.scalar.copy, xq, 1, X_SPLIT, N)
+        quantize(xq)
+        interleave(nc.scalar.copy, w1q, 0, 0, M)
+        quantize(w1q)
         interleave(nc.scalar.copy, w2q, 0, 0, M)
+        nc.vector.transpose(out=feat_cols[:], in_=feat_rows[:])
+        quantize(w2q)
         nc.vector.tensor_tensor(
             out=gain[:], in0=feat_cols[:, 0:M:32], in1=feat_cols[:, M : 2 * M : 32], op=ALU.mult
         )
-        quantize(w2q, 0)
-        for h in range(2):
-            interleave(nc.vector.tensor_copy, dxq, h, 0, HALF)
-            quantize(dxq, h)
+        interleave(nc.vector.tensor_copy, dxq, 0, 0, N)
+        interleave(nc.vector.tensor_copy, dxq, 1, 0, X_SPLIT)
 
         def so_col(g):
             return feat_cols[:, 32 * g : 32 * g + 1]
@@ -126,6 +122,9 @@ def tile_rows_tnagree_kernel(tc, x, w1, w2, so, dx, og, base, out):
         for g in range(G):
             product(bank1[g], w1q, xq, g)
             nc.scalar.copy(out=z1[g][:], in_=bank1[g][:])
+            if g == 0:
+                interleave(nc.scalar.copy, dxq, 1, X_SPLIT, N)
+        quantize(dxq)
         for g in range(G):
             product(bank2[g], w2q, xq, g)
             nc.vector.tensor_tensor(out=prod[g][:], in0=bank2[g][:], in1=z1[g][:], op=ALU.mult)

@@ -16,8 +16,10 @@ ALU = mybir.AluOpType
 P = 128
 PACK = 4
 ROWS = D // PACK
-HALF = N // 2
-X_SPLIT = 344
+BLOCK = 32
+RUN = 4
+VECTOR_COLS = 344
+LAST = G - 1
 
 
 def tile_rows_tnagree_kernel(tc, x, w1, w2, so, dx, og, base, out):
@@ -28,69 +30,79 @@ def tile_rows_tnagree_kernel(tc, x, w1, w2, so, dx, og, base, out):
         ctx.enter_context(tc.manual_schedule())
 
         def operand(name, width, parts):
-            raws = [
-                sb.tile([P, PACK // parts, width], F32, name=name + "_raw" + str(h), align_bytes=64)
-                for h in range(parts)
-            ]
-            grouped = sb.tile([P, width, PACK], BF16, name=name + "_bf", align_bytes=64)
-            codes = sb.tile([P, width], U32, name=name + "_codes", align_bytes=64)
-            scales = sb.tile([P, width], U8, name=name + "_scales", align_bytes=64)
-            return raws, grouped, codes, scales
+            return {
+                "raw": [
+                    sb.tile([P, PACK // parts, width], F32, name=name + "_raw" + str(h), align_bytes=64)
+                    for h in range(parts)
+                ],
+                "rounded": sb.tile([P, width, PACK], BF16, name=name + "_rounded", align_bytes=64),
+                "codes": sb.tile([P, width], U32, name=name + "_codes", align_bytes=64),
+                "scales": sb.tile([P, width], U8, name=name + "_scales", align_bytes=64),
+            }
 
-        xq, dxq = operand("x", N, 2), operand("dx", N, 2)
-        w1q, w2q = operand("w1", M, 1), operand("w2", M, 1)
+        def places(opnd, h):
+            count = PACK // len(opnd["raw"])
+            return slice(h * count, (h + 1) * count)
 
         def load(src, opnd, h):
-            places = opnd[0][h].shape[1]
             rows = src.rearrange("g (p j) n -> (g p) j n", j=PACK)
-            nc.sync.dma_start(out=opnd[0][h][:], in_=rows[:, h * places : (h + 1) * places, :])
+            nc.sync.dma_start(out=opnd["raw"][h][:], in_=rows[:, places(opnd, h), :])
 
         def interleave(copy, opnd, h, c0, c1):
-            places = opnd[0][h].shape[1]
             copy(
-                out=opnd[1][:, c0:c1, h * places : (h + 1) * places].rearrange("p (c i) j -> p c j i", i=4),
-                in_=opnd[0][h][:, :, c0:c1].rearrange("p j (c i) -> p c j i", i=4),
+                out=opnd["rounded"][:, c0:c1, places(opnd, h)].rearrange("p (c i) j -> p c j i", i=RUN),
+                in_=opnd["raw"][h][:, :, c0:c1].rearrange("p j (c i) -> p c j i", i=RUN),
             )
 
         def quantize(opnd):
             nc.vector.quantize_mx(
-                out=opnd[2][:].bitcast(FP8X4),
-                scales=opnd[3][:],
-                in_=opnd[1][:].rearrange("p n j -> p (n j)"),
+                out=opnd["codes"][:].bitcast(FP8X4),
+                scales=opnd["scales"][:],
+                in_=opnd["rounded"][:].rearrange("p n j -> p (n j)"),
             )
 
-        def product(bank, w, act, g):
+        def product(bank, weights, inputs, g):
             rows = slice(ROWS * g, ROWS * (g + 1))
             nc.tensor.matmul_mx(
                 out=bank[:],
-                lhsT=w[2][rows, :].bitcast(FP8X4),
-                lhsT_scale=w[3][rows, :],
-                rhs=act[2][rows, :].bitcast(FP8X4),
-                rhs_scale=act[3][rows, :],
+                lhsT=weights["codes"][rows, :].bitcast(FP8X4),
+                lhsT_scale=weights["scales"][rows, :],
+                rhs=inputs["codes"][rows, :].bitcast(FP8X4),
+                rhs_scale=inputs["scales"][rows, :],
                 start=True,
                 stop=True,
             )
 
         def per_group(name):
-            return [sb.tile([P, N], F32, name=name + str(g), align_bytes=64) for g in range(G)]
+            return [sb.tile([P, N], F32, name=name + "_" + str(g), align_bytes=64) for g in range(G)]
+
+        xq, dxq = operand("x", N, 2), operand("dx", N, 2)
+        w1q, w2q = operand("w1", M, 1), operand("w2", M, 1)
 
         bank1 = [ps.tile([M, N], F32, name="bank1_" + str(g)) for g in range(G)]
         bank2 = [ps.tile([M, N], F32, name="bank2_" + str(g)) for g in range(G)]
-        z1, z2, prod, sq, lg = (per_group(n) for n in ("z1_", "z2_", "prod", "sq", "lg"))
-        u, v, tp, r3, t, y = (per_group(n) for n in ("u", "v", "tp", "r3_", "t", "y"))
+        z1, z2, prod, prod_sq, log_nm2, weight = (
+            per_group(name) for name in ("z1", "z2", "prod", "prod_sq", "log_nm2", "weight")
+        )
+        tz1_z2, tz2_z1, tangent, change, result = (
+            per_group(name) for name in ("tz1_z2", "tz2_z1", "tangent", "change", "result")
+        )
         base_sb = sb.tile([P, G, N], F32)
+
         feat_rows = sb.tile([P, 2 * M], F32, align_bytes=64)
         feat_cols = sb.tile([P, 2 * M], F32, align_bytes=64)
-        gain = sb.tile([P, G], F32)
-        warm = sb.tile([P, 8], F32)
+        log_so_rows = sb.tile([P, M], F32, align_bytes=64)
+        log_so_cols = sb.tile([P, M], F32, align_bytes=64)
 
-        nc.vector.memset(feat_rows[:], 0.0)
-        nc.vector.memset(warm[:], 1.0)
+        def column(cols, first, g):
+            return cols[:, first + BLOCK * g : first + BLOCK * g + 1]
+
+        nc.vector.memset(feat_rows[:], 1.0)
         load(x, xq, 0)
         for k, vec in enumerate((so, og)):
             nc.sync.dma_start(
-                out=feat_rows[0:P:32, k * M : (k + 1) * M].rearrange("q (g i) -> q g i", g=G),
-                in_=vec.rearrange("g (q i) o -> q g (i o)", i=32),
+                out=feat_rows[0:P:BLOCK, k * M : (k + 1) * M].rearrange("q (g i) -> q g i", g=G),
+                in_=vec.rearrange("g (q i) o -> q g (i o)", i=BLOCK),
             )
         load(x, xq, 1)
         load(w1, w1q, 0)
@@ -99,88 +111,77 @@ def tile_rows_tnagree_kernel(tc, x, w1, w2, so, dx, og, base, out):
         load(dx, dxq, 1)
         nc.sync.dma_start(out=base_sb[:], in_=base.rearrange("g m n -> m g n"))
 
-        nc.scalar.activation(out=warm[:, 4:5], in_=warm[:, 0:1], func=ACT.Ln)
+        nc.scalar.activation(out=log_so_rows[:], in_=feat_rows[:, 0:M], func=ACT.Ln)
 
         interleave(nc.vector.tensor_copy, xq, 0, 0, N)
-        interleave(nc.vector.tensor_copy, xq, 1, 0, X_SPLIT)
-        interleave(nc.scalar.copy, xq, 1, X_SPLIT, N)
+        interleave(nc.vector.tensor_copy, xq, 1, 0, N)
         quantize(xq)
         interleave(nc.scalar.copy, w1q, 0, 0, M)
         quantize(w1q)
         interleave(nc.scalar.copy, w2q, 0, 0, M)
         nc.vector.transpose(out=feat_cols[:], in_=feat_rows[:])
+        nc.vector.transpose(out=log_so_cols[:], in_=log_so_rows[:])
         quantize(w2q)
-        nc.vector.tensor_tensor(
-            out=gain[:], in0=feat_cols[:, 0:M:32], in1=feat_cols[:, M : 2 * M : 32], op=ALU.mult
-        )
         interleave(nc.vector.tensor_copy, dxq, 0, 0, N)
-        interleave(nc.vector.tensor_copy, dxq, 1, 0, X_SPLIT)
-
-        def so_col(g):
-            return feat_cols[:, 32 * g : 32 * g + 1]
+        interleave(nc.vector.tensor_copy, dxq, 1, 0, VECTOR_COLS)
 
         for g in range(G):
             product(bank1[g], w1q, xq, g)
             nc.scalar.copy(out=z1[g][:], in_=bank1[g][:])
             if g == 0:
-                interleave(nc.scalar.copy, dxq, 1, X_SPLIT, N)
+                interleave(nc.scalar.copy, dxq, 1, VECTOR_COLS, N)
         quantize(dxq)
         for g in range(G):
             product(bank2[g], w2q, xq, g)
             nc.vector.tensor_tensor(out=prod[g][:], in0=bank2[g][:], in1=z1[g][:], op=ALU.mult)
             nc.scalar.copy(out=z2[g][:], in_=bank2[g][:])
 
-        def cross(g):
-            for banks, w, z, dst in ((bank1, w1q, z2, v), (bank2, w2q, z1, u)):
-                product(banks[g], w, dxq, g)
-                nc.vector.tensor_tensor(out=dst[g][:], in0=banks[g][:], in1=z[g][:], op=ALU.mult)
+        for g in range(G):
+            product(bank1[g], w1q, dxq, g)
+            nc.vector.tensor_tensor(out=tz1_z2[g][:], in0=bank1[g][:], in1=z2[g][:], op=ALU.mult)
+            product(bank2[g], w2q, dxq, g)
+            nc.vector.tensor_tensor(out=tz2_z1[g][:], in0=bank2[g][:], in1=z1[g][:], op=ALU.mult)
+
+        for g in range(LAST):
+            nc.gpsimd.tensor_tensor(out=prod_sq[g][:], in0=prod[g][:], in1=prod[g][:], op=ALU.mult)
+        for g in range(G):
+            engine = nc.gpsimd if g == 0 else nc.vector
+            engine.tensor_tensor(out=tangent[g][:], in0=tz2_z1[g][:], in1=tz1_z2[g][:], op=ALU.add)
 
         def logarithm(g):
-            nc.scalar.activation(out=lg[g][:], in_=sq[g][:], func=ACT.Ln, bias=so_col(g))
+            nc.scalar.activation(
+                out=log_nm2[g][:], in_=prod_sq[g][:], func=ACT.Ln, bias=column(feat_cols, 0, g)
+            )
 
-        def power(g):
-            nc.scalar.activation(out=r3[g][:], in_=lg[g][:], func=ACT.Exp, scale=-1.5)
-
-        def tangent_sum(engine, g):
-            engine.tensor_tensor(out=tp[g][:], in0=u[g][:], in1=v[g][:], op=ALU.add)
-
-        for g in range(G):
-            cross(g)
-
-        for g in range(G - 1):
-            nc.gpsimd.tensor_tensor(out=sq[g][:], in0=prod[g][:], in1=prod[g][:], op=ALU.mult)
         logarithm(0)
-        nc.scalar.activation(out=sq[G - 1][:], in_=prod[G - 1][:], func=ACT.Square)
+        nc.scalar.activation(out=prod_sq[LAST][:], in_=prod[LAST][:], func=ACT.Square)
         logarithm(1)
-        logarithm(3)
-        logarithm(2)
+        logarithm(LAST)
+        logarithm(LAST - 1)
         for g in range(G):
-            power(g)
-        for g in range(G):
-            tangent_sum(nc.gpsimd if g < 2 else nc.vector, g)
+            nc.scalar.activation(
+                out=weight[g][:], in_=log_nm2[g][:], func=ACT.Exp, scale=-1.5, bias=column(log_so_cols, 0, g)
+            )
 
         def weigh(g, c0, c1):
             nc.vector.scalar_tensor_tensor(
-                out=t[g][:, c0:c1],
-                in0=tp[g][:, c0:c1],
-                scalar=gain[:, g : g + 1],
-                in1=r3[g][:, c0:c1],
+                out=change[g][:, c0:c1],
+                in0=tangent[g][:, c0:c1],
+                scalar=column(feat_cols, M, g),
+                in1=weight[g][:, c0:c1],
                 op0=ALU.mult,
                 op1=ALU.mult,
             )
 
         def finish(g, c0, c1):
-            nc.vector.tensor_tensor(out=y[g][:, c0:c1], in0=t[g][:, c0:c1], in1=base_sb[:, g, c0:c1], op=ALU.add)
-            nc.sync.dma_start(out=out[g, :, c0:c1], in_=y[g][:, c0:c1])
+            nc.vector.tensor_tensor(
+                out=result[g][:, c0:c1], in0=change[g][:, c0:c1], in1=base_sb[:, g, c0:c1], op=ALU.add
+            )
+            nc.sync.dma_start(out=out[g, :, c0:c1], in_=result[g][:, c0:c1])
 
-        last = G - 1
-        weigh(0, 0, N)
-        for g in range(last):
-            if g + 1 < last:
-                weigh(g + 1, 0, N)
-            else:
-                weigh(last, 0, HALF)
-            finish(g, 0, N)
-        weigh(last, HALF, N)
-        finish(last, 0, HALF)
-        finish(last, HALF, N)
+        pieces = [(g, 0, N) for g in range(LAST)] + [(LAST, 0, N // 2), (LAST, N // 2, N)]
+        weigh(*pieces[0])
+        for k, piece in enumerate(pieces):
+            if k + 1 < len(pieces):
+                weigh(*pieces[k + 1])
+            finish(*piece)

from contextlib import ExitStack

import concourse.mybir as mybir

G, D, M, N = 4, 128, 128, 512
FLOPS = 4 * 2 * G * D * M * N

F32 = mybir.dt.float32
BF16 = mybir.dt.bfloat16
U32 = mybir.dt.uint32
U8 = mybir.dt.uint8
FP8X4 = mybir.dt.float8_e4m3fn_x4
ACT = mybir.ActivationFunctionType
ALU = mybir.AluOpType

P = 128
PACK = 4
ROWS = D // PACK
BLOCK = 32
RUN = 4
VECTOR_COLS = 344
LAST = G - 1


def tile_rows_tnagree_kernel(tc, x, w1, w2, so, dx, og, base, out):
    nc = tc.nc
    with ExitStack() as ctx:
        sb = ctx.enter_context(tc.tile_pool(name="sb", bufs=1))
        ps = ctx.enter_context(tc.psum_pool(name="ps", bufs=1))
        ctx.enter_context(tc.manual_schedule())

        def operand(name, width, parts):
            return {
                "raw": [
                    sb.tile([P, PACK // parts, width], F32, name=name + "_raw" + str(h), align_bytes=64)
                    for h in range(parts)
                ],
                "rounded": sb.tile([P, width, PACK], BF16, name=name + "_rounded", align_bytes=64),
                "codes": sb.tile([P, width], U32, name=name + "_codes", align_bytes=64),
                "scales": sb.tile([P, width], U8, name=name + "_scales", align_bytes=64),
            }

        def places(opnd, h):
            count = PACK // len(opnd["raw"])
            return slice(h * count, (h + 1) * count)

        def load(src, opnd, h):
            rows = src.rearrange("g (p j) n -> (g p) j n", j=PACK)
            nc.sync.dma_start(out=opnd["raw"][h][:], in_=rows[:, places(opnd, h), :])

        def interleave(copy, opnd, h, c0, c1):
            copy(
                out=opnd["rounded"][:, c0:c1, places(opnd, h)].rearrange("p (c i) j -> p c j i", i=RUN),
                in_=opnd["raw"][h][:, :, c0:c1].rearrange("p j (c i) -> p c j i", i=RUN),
            )

        def quantize(opnd):
            nc.vector.quantize_mx(
                out=opnd["codes"][:].bitcast(FP8X4),
                scales=opnd["scales"][:],
                in_=opnd["rounded"][:].rearrange("p n j -> p (n j)"),
            )

        def product(bank, weights, inputs, g):
            rows = slice(ROWS * g, ROWS * (g + 1))
            nc.tensor.matmul_mx(
                out=bank[:],
                lhsT=weights["codes"][rows, :].bitcast(FP8X4),
                lhsT_scale=weights["scales"][rows, :],
                rhs=inputs["codes"][rows, :].bitcast(FP8X4),
                rhs_scale=inputs["scales"][rows, :],
                start=True,
                stop=True,
            )

        def per_group(name):
            return [sb.tile([P, N], F32, name=name + "_" + str(g), align_bytes=64) for g in range(G)]

        xq, dxq = operand("x", N, 2), operand("dx", N, 2)
        w1q, w2q = operand("w1", M, 1), operand("w2", M, 1)

        bank1 = [ps.tile([M, N], F32, name="bank1_" + str(g)) for g in range(G)]
        bank2 = [ps.tile([M, N], F32, name="bank2_" + str(g)) for g in range(G)]
        z1, z2, prod, prod_sq, log_nm2, weight = (
            per_group(name) for name in ("z1", "z2", "prod", "prod_sq", "log_nm2", "weight")
        )
        tz1_z2, tz2_z1, tangent, change, result = (
            per_group(name) for name in ("tz1_z2", "tz2_z1", "tangent", "change", "result")
        )
        base_sb = sb.tile([P, G, N], F32)

        feat_rows = sb.tile([P, 2 * M], F32, align_bytes=64)
        feat_cols = sb.tile([P, 2 * M], F32, align_bytes=64)
        log_so_rows = sb.tile([P, M], F32, align_bytes=64)
        log_so_cols = sb.tile([P, M], F32, align_bytes=64)

        def column(cols, first, g):
            return cols[:, first + BLOCK * g : first + BLOCK * g + 1]

        nc.vector.memset(feat_rows[:], 1.0)
        load(x, xq, 0)
        for k, vec in enumerate((so, og)):
            nc.sync.dma_start(
                out=feat_rows[0:P:BLOCK, k * M : (k + 1) * M].rearrange("q (g i) -> q g i", g=G),
                in_=vec.rearrange("g (q i) o -> q g (i o)", i=BLOCK),
            )
        load(x, xq, 1)
        load(w1, w1q, 0)
        load(w2, w2q, 0)
        load(dx, dxq, 0)
        load(dx, dxq, 1)
        nc.sync.dma_start(out=base_sb[:], in_=base.rearrange("g m n -> m g n"))

        nc.scalar.activation(out=log_so_rows[:], in_=feat_rows[:, 0:M], func=ACT.Ln)

        interleave(nc.vector.tensor_copy, xq, 0, 0, N)
        interleave(nc.vector.tensor_copy, xq, 1, 0, N)
        quantize(xq)
        interleave(nc.scalar.copy, w1q, 0, 0, M)
        quantize(w1q)
        interleave(nc.scalar.copy, w2q, 0, 0, M)
        nc.vector.transpose(out=feat_cols[:], in_=feat_rows[:])
        nc.vector.transpose(out=log_so_cols[:], in_=log_so_rows[:])
        quantize(w2q)
        interleave(nc.vector.tensor_copy, dxq, 0, 0, N)
        interleave(nc.vector.tensor_copy, dxq, 1, 0, VECTOR_COLS)

        for g in range(G):
            product(bank1[g], w1q, xq, g)
            nc.scalar.copy(out=z1[g][:], in_=bank1[g][:])
            if g == 0:
                interleave(nc.scalar.copy, dxq, 1, VECTOR_COLS, N)
        quantize(dxq)
        for g in range(G):
            product(bank2[g], w2q, xq, g)
            nc.vector.tensor_tensor(out=prod[g][:], in0=bank2[g][:], in1=z1[g][:], op=ALU.mult)
            nc.scalar.copy(out=z2[g][:], in_=bank2[g][:])

        for g in range(G):
            product(bank1[g], w1q, dxq, g)
            nc.vector.tensor_tensor(out=tz1_z2[g][:], in0=bank1[g][:], in1=z2[g][:], op=ALU.mult)
            product(bank2[g], w2q, dxq, g)
            nc.vector.tensor_tensor(out=tz2_z1[g][:], in0=bank2[g][:], in1=z1[g][:], op=ALU.mult)

        for g in range(LAST):
            nc.gpsimd.tensor_tensor(out=prod_sq[g][:], in0=prod[g][:], in1=prod[g][:], op=ALU.mult)
        for g in range(G):
            engine = nc.gpsimd if g == 0 else nc.vector
            engine.tensor_tensor(out=tangent[g][:], in0=tz2_z1[g][:], in1=tz1_z2[g][:], op=ALU.add)

        def logarithm(g):
            nc.scalar.activation(
                out=log_nm2[g][:], in_=prod_sq[g][:], func=ACT.Ln, bias=column(feat_cols, 0, g)
            )

        logarithm(0)
        nc.scalar.activation(out=prod_sq[LAST][:], in_=prod[LAST][:], func=ACT.Square)
        logarithm(1)
        logarithm(LAST)
        logarithm(LAST - 1)
        for g in range(G):
            nc.scalar.activation(
                out=weight[g][:], in_=log_nm2[g][:], func=ACT.Exp, scale=-1.5, bias=column(log_so_cols, 0, g)
            )

        def weigh(g, c0, c1):
            nc.vector.scalar_tensor_tensor(
                out=change[g][:, c0:c1],
                in0=tangent[g][:, c0:c1],
                scalar=column(feat_cols, M, g),
                in1=weight[g][:, c0:c1],
                op0=ALU.mult,
                op1=ALU.mult,
            )

        def finish(g, c0, c1):
            nc.vector.tensor_tensor(
                out=result[g][:, c0:c1], in0=change[g][:, c0:c1], in1=base_sb[:, g, c0:c1], op=ALU.add
            )
            nc.sync.dma_start(out=out[g, :, c0:c1], in_=result[g][:, c0:c1])

        pieces = [(g, 0, N) for g in range(LAST)] + [(LAST, 0, N // 2), (LAST, N // 2, N)]
        weigh(*pieces[0])
        for k, piece in enumerate(pieces):
            if k + 1 < len(pieces):
                weigh(*pieces[k + 1])
            finish(*piece)
